import numpy as np
import ml_dtypes


def mxq(x, axis, fmt="e4m3"):
    dtype, down = {"e4m3": (ml_dtypes.float8_e4m3fn, 7), "e5m2": (ml_dtypes.float8_e5m2, 14)}[fmt]
    v = np.moveaxis(np.asarray(x, np.float32).astype(ml_dtypes.bfloat16).astype(np.float64), axis, -1)
    blocks = v.reshape(v.shape[:-1] + (-1, 32))
    amax = np.abs(blocks).max(-1, keepdims=True)
    byte = np.maximum(np.where(amax > 0, np.frexp(amax)[1] - 1 + 127, 0) - down, 1)
    scale = np.exp2(byte - 127.0)
    codes = (blocks / scale).astype(np.float32).astype(dtype).astype(np.float64)
    return np.moveaxis((codes * scale).reshape(v.shape), -1, axis)


WIDE = False


def mx_kscale(k):
    if not WIDE:
        return np.ones(k)
    levels = np.array([10, -10, 5, -5, 0])
    if k % 512:
        return np.exp2(np.random.permutation(np.resize(levels, k // 32))).repeat(32)
    a = np.empty((k // 512, 16))
    for p in range(k // 512):
        a[p, :8] = np.random.permutation(np.resize(levels, 8))
        for g in range(8):
            far = levels[np.abs(levels - a[p, g]) >= 10]
            a[p, g + 8] = far[np.random.randint(len(far))]
    return np.exp2(a.ravel()).repeat(32)


def f64(x):
    return np.asarray(x).astype(np.float64)


def striped8(idx):
    return np.asarray(idx).reshape(8, -1, 16).transpose(0, 2, 1).reshape(128, -1).astype(np.uint16)


def unstriped8(offs):
    return offs.reshape(8, 16, -1).transpose(0, 2, 1).reshape(8, -1).astype(np.int64)


def pick8(x, idx, run):
    r = np.arange(len(x))
    return x[r[:, None], idx[r % (8 * run) // run]]


E2M1 = np.array([0.0, 0.5, 1.0, 1.5, 2.0, 3.0, 4.0, 6.0, -0.0, -0.5, -1.0, -1.5, -2.0, -3.0, -4.0, -6.0])


def pack_weight(w, fmt):
    k, n = w.shape
    w = f64(np.asarray(w, np.float32).astype(ml_dtypes.bfloat16)).reshape(k // 32, 32, n)
    amax = np.abs(w).max(1)
    if fmt == "e4m3":
        byte = np.frexp(amax)[1] - 1 + 127 - 7
    else:
        mant, ex = np.frexp(amax / 6.0)
        byte = np.where(mant > 0.5, ex, ex - 1) + 127
    byte = np.clip(np.where(amax > 0, byte, 1), 1, 254)
    scaled = (w * np.exp2(127.0 - byte)[:, None, :]).reshape(k, n).astype(np.float32)
    by_word = np.ascontiguousarray(scaled.reshape(k // 512, 128, 4, n).transpose(0, 1, 3, 2))
    if fmt == "e4m3":
        words = by_word.astype(ml_dtypes.float8_e4m3fn).view(np.uint8)
    else:
        c = by_word.astype(ml_dtypes.float4_e2m1fn).view(np.uint8) & 0xF
        words = (c[..., 0::2] | (c[..., 1::2] << 4)).reshape(k // 512, 128, 2 * n)
    return np.ascontiguousarray(words), np.ascontiguousarray(byte.astype(np.uint8).reshape(k // 512, 16, n))


def unpack_weight(words, scales, fmt):
    g, _, n = scales.shape
    words = np.ascontiguousarray(words).reshape(g, 128, n, -1)
    if fmt == "e4m3":
        vals = words.view(ml_dtypes.float8_e4m3fn).astype(np.float64)
    else:
        nib = np.empty((g, 128, n, 4), np.uint8)
        nib[..., 0::2] = words & 0xF
        nib[..., 1::2] = words >> 4
        vals = E2M1[nib]
    vals = vals * np.repeat(np.exp2(scales.astype(np.float64) - 127.0), 8, axis=1)[..., None]
    return vals.transpose(0, 1, 3, 2).reshape(g * 512, n)


D, K, T, U, X, I, Q = 512, 512, 1024, 1024, 1024, 512, 128


def setup_inputs():
    n = np.random.standard_normal
    idx = np.stack([np.random.permutation(T)[:I] for _ in range(8)])
    idx2 = np.stack([np.random.permutation(U)[:I] for _ in range(8)])
    idx3 = np.stack([np.random.permutation(X)[:I] for _ in range(8)])
    idx4 = np.stack([np.random.permutation(T)[:I] for _ in range(8)])
    idx5 = np.stack([np.random.permutation(U)[:I] for _ in range(8)])
    idx6 = np.stack([np.random.permutation(X)[:I] for _ in range(8)])
    fd = mx_kscale(D)
    fk = mx_kscale(K)
    wqp = pack_weight(n((D, K)) * 1.0 / np.sqrt(D) * fd[:, None] * fk, "e4m3")
    keysp = pack_weight(n((K, T)) * 1.0 / np.sqrt(K) / fk[:, None], "e4m3")
    notesp = pack_weight(n((K, U)) * 1.0 / np.sqrt(K) / fk[:, None], "e2m1")
    usersp = pack_weight(n((D, X)) * 1.0 / np.sqrt(D) * fd[:, None], "e4m3")
    return {
        "states": (n((D, Q)) * 0.95 / fd[:, None]).astype(np.float32),
        "wq_words": wqp[0],
        "wq_scales": wqp[1],
        "keys_words": keysp[0],
        "keys_scales": keysp[1],
        "notes_words": notesp[0],
        "notes_scales": notesp[1],
        "users_words": usersp[0],
        "users_scales": usersp[1],
        "offs": striped8(idx),
        "offs2": striped8(idx2),
        "offs3": striped8(idx3),
        "offs4": striped8(idx4),
        "offs5": striped8(idx5),
        "offs6": striped8(idx6),
    }


def reference(states, wq_words, wq_scales, keys_words, keys_scales, notes_words, notes_scales, users_words, users_scales, offs, offs2, offs3, offs4, offs5, offs6):
    idx = unstriped8(offs)
    idx2 = unstriped8(offs2)
    idx3 = unstriped8(offs3)
    idx4 = unstriped8(offs4)
    idx5 = unstriped8(offs5)
    idx6 = unstriped8(offs6)
    wqu = unpack_weight(wq_words, wq_scales, "e4m3")
    keysu = unpack_weight(keys_words, keys_scales, "e4m3")
    notesu = unpack_weight(notes_words, notes_scales, "e2m1")
    usersu = unpack_weight(users_words, users_scales, "e4m3")
    statesq = mxq(f64(states), 0, "e4m3")
    qv = wqu.T @ statesq
    qvq = mxq(qv, 0, "e4m3")
    a = qvq.T @ keysu
    b = qvq.T @ notesu
    c0 = statesq.T @ usersu
    f1 = np.zeros((Q, U))
    f1[np.arange(Q)[:, None], idx2[np.arange(Q) % 128 // 16]] = pick8(a, idx, 16)
    f2 = np.zeros((Q, X))
    f2[np.arange(Q)[:, None], idx3[np.arange(Q) % 128 // 16]] = pick8(b, idx2, 16)
    f3 = np.zeros((Q, T))
    f3[np.arange(Q)[:, None], idx[np.arange(Q) % 128 // 16]] = pick8(c0, idx3, 16)
    aa = a + f3
    bb = b + f1
    cc = c0 - f2
    v = np.maximum(pick8(aa, idx4, 16), pick8(bb, idx5, 16))
    y = v - pick8(cc, idx6, 16)
    return y

@@ -1,0 +1,169 @@
+from contextlib import ExitStack
+
+import concourse.mybir as mybir
+
+D, K, T, I, Q = 512, 512, 1024, 512, 128
+FLOPS = 2 * Q * (D * K + 3 * 512 * T)
+
+F32 = mybir.dt.float32
+BF16 = mybir.dt.bfloat16
+I32 = mybir.dt.int32
+U32 = mybir.dt.uint32
+U16 = mybir.dt.uint16
+U8 = mybir.dt.uint8
+FP8X4 = mybir.dt.float8_e4m3fn_x4
+FP4X4 = mybir.dt.float4_e2m1fn_x4
+COPY = mybir.ActivationFunctionType.Copy
+ALU = mybir.AluOpType
+
+P = 128
+PACK = 4
+BANK = 512
+PER_COLUMN = 16
+
+
+def tile_attend_rotation_madethree_kernel(
+    tc, states, wq_words, wq_scales, keys_words, keys_scales, notes_words, notes_scales,
+    users_words, users_scales, offs, offs2, offs3, offs4, offs5, offs6, out,
+):
+    nc = tc.nc
+    with ExitStack() as ctx:
+        sb = ctx.enter_context(tc.tile_pool(name="sb", bufs=1))
+        ps = ctx.enter_context(tc.psum_pool(name="ps", bufs=1))
+
+        def load_list(src, name):
+            tile = sb.tile([P, I // PER_COLUMN], U16, name=name)
+            nc.sync.dma_start(tile[:], src)
+            return tile
+
+        def load_plane(queue, plane, src):
+            for r in range(4):
+                queue.dma_start(plane[r:P:32, :].bitcast(I32), src[0, r:16:4, :].bitcast(I32))
+
+        def load_words(src, columns, name):
+            tile = sb.tile([P, columns], U32, name=name, align_bytes=64)
+            nc.sync.dma_start(tile[:].bitcast(I32), src[0].rearrange("p n t -> p (n t)").bitcast(I32))
+            return tile
+
+        def slots(lst, first, count):
+            return lst[:, first // PER_COLUMN : (first + count) // PER_COLUMN]
+
+        users_plane = sb.tile([P, T], U8, align_bytes=64)
+        wq_plane = sb.tile([P, K], U8, align_bytes=64)
+        keys_plane = sb.tile([P, T], U8, align_bytes=64)
+        notes_plane = sb.tile([P, T], U8, align_bytes=64)
+        nc.vector.memset(wq_plane[:].bitcast(U32), 0)
+        f3 = sb.tile([P, T], F32)
+        f1 = sb.tile([P, T], F32)
+        f2 = sb.tile([P, T], F32)
+        for window in (f3, f1, f2):
+            nc.vector.memset(window[:], 0.0)
+
+        states_raw = sb.tile([P, PACK, Q], F32)
+        nc.sync.dma_start(states_raw[:], states.rearrange("(p j) q -> p j q", j=PACK))
+        load_plane(nc.scalar, users_plane, users_scales)
+        users_codes = load_words(users_words, T, "users_codes")
+        wq_codes = load_words(wq_words, K, "wq_codes")
+        load_plane(nc.sync, wq_plane, wq_scales)
+        idx3 = load_list(offs3, "idx3")
+        idx = load_list(offs, "idx")
+        keys_codes = load_words(keys_words, T, "keys_codes")
+        load_plane(nc.sync, keys_plane, keys_scales)
+        idx2 = load_list(offs2, "idx2")
+        notes_codes = sb.tile([P, 2 * T], U8, align_bytes=64)
+        nc.sync.dma_start(notes_codes[:].bitcast(I32), notes_words[0].bitcast(I32))
+        load_plane(nc.sync, notes_plane, notes_scales)
+        idx4 = load_list(offs4, "idx4")
+        idx5 = load_list(offs5, "idx5")
+        idx6 = load_list(offs6, "idx6")
+
+        states_bf = sb.tile([P, Q, PACK], BF16, align_bytes=64)
+        nc.vector.tensor_copy(states_bf[:], states_raw[:].rearrange("p j q -> p q j"))
+        states_codes = sb.tile([P, Q], U32, align_bytes=64)
+        states_plane = sb.tile([P, Q], U8, align_bytes=64)
+        nc.vector.quantize_mx(
+            out=states_codes[:].bitcast(FP8X4),
+            scales=states_plane[:],
+            in_=states_bf[:].rearrange("p q j -> p (q j)"),
+        )
+
+        def score(name, lhs_codes, lhs_plane, rhs_of_bank, rhs_plane):
+            scores = sb.tile([P, T], F32, name=name)
+            banks = []
+            for h in range(T // BANK):
+                cols = slice(h * BANK, (h + 1) * BANK)
+                bank = ps.tile([P, BANK], F32, name=f"{name}_bank{h}")
+                nc.tensor.matmul_mx(
+                    out=bank[:], lhsT=lhs_codes[:].bitcast(FP8X4), lhsT_scale=lhs_plane[:],
+                    rhs=rhs_of_bank(cols), rhs_scale=rhs_plane[:, cols], start=True, stop=True,
+                )
+                nc.scalar.activation(scores[:, cols], bank[:], COPY)
+                banks.append(bank)
+            return scores, banks
+
+        def gather(name, window, lst, first, count):
+            picked = sb.tile([P, count], F32, name=name)
+            nc.scalar.activation(picked[:], window[:].indirect(slots(lst, first, count)), COPY)
+            return picked
+
+        def scatter(window, lst, first, values):
+            nc.vector.tensor_copy(window[:].indirect(slots(lst, first, values.shape[1])), values)
+
+        half = I // 2
+        quarter = I // 4
+
+        c0, c0_banks = score("c0", states_codes, states_plane, lambda cols: users_codes[:, cols].bitcast(FP8X4), users_plane)
+
+        wq_dealt = sb.tile([P, PACK, P], U32, align_bytes=64)
+        nc.vector.tensor_copy(wq_dealt[:].rearrange("p j m -> p m j"), wq_codes[:].rearrange("p (m j) -> p m j", j=PACK))
+        wq_plane_dealt = sb.tile([P, PACK, P], U8, align_bytes=64)
+        nc.vector.tensor_copy(wq_plane_dealt[:].rearrange("p j m -> p m j"), wq_plane[:].rearrange("p (m j) -> p m j", j=PACK))
+        qv_bank = ps.tile([P, PACK, Q], F32)
+        for j in range(PACK):
+            nc.tensor.matmul_mx(
+                out=qv_bank[:, j, :], lhsT=wq_dealt[:, j, :].bitcast(FP8X4), lhsT_scale=wq_plane_dealt[:, j, :],
+                rhs=states_codes[:].bitcast(FP8X4), rhs_scale=states_plane[:], start=True, stop=True,
+            )
+
+        c0_first = gather("c0_first", c0, idx3, 0, half)
+        qv_bf = sb.tile([P, Q, PACK], BF16, align_bytes=64)
+        nc.scalar.copy(qv_bf[:], qv_bank[:].rearrange("p j q -> p q j"))
+        scatter(f3, idx, 0, c0_first[:, :quarter])
+        qv_codes = sb.tile([P, Q], U32, align_bytes=64)
+        qv_plane = sb.tile([P, Q], U8, align_bytes=64)
+        nc.vector.quantize_mx(
+            out=qv_codes[:].bitcast(FP8X4),
+            scales=qv_plane[:],
+            in_=qv_bf[:].rearrange("p q j -> p (q j)"),
+        )
+        scatter(f3, idx, quarter, c0_first[:, quarter:])
+        c0_second = gather("c0_second", c0, idx3, half, half)
+        scatter(f3, idx, half, c0_second[:])
+
+        a, a_banks = score("a", qv_codes, qv_plane, lambda cols: keys_codes[:, cols].bitcast(FP8X4), keys_plane)
+        for h in range(2):
+            picked = gather(f"a_picked{h}", a, idx, h * half, half)
+            scatter(f1, idx2, h * half, picked[:])
+        aa = sb.tile([P, T], F32)
+        nc.gpsimd.tensor_tensor(aa[:], a[:], f3[:], ALU.add)
+
+        b, b_banks = score("b", qv_codes, qv_plane, lambda cols: notes_codes[:, 2 * cols.start : 2 * cols.stop].bitcast(FP4X4), notes_plane)
+        for h in range(2):
+            picked = gather(f"b_picked{h}", b, idx2, h * half, half)
+            scatter(f2, idx3, h * half, picked[:])
+        bb = sb.tile([P, T], F32)
+        nc.gpsimd.tensor_tensor(bb[:], b[:], f1[:], ALU.add)
+
+        aa_picked = gather("aa_picked", aa, idx4, 0, I)
+        bb_picked = gather("bb_picked", bb, idx5, 0, I)
+
+        cc = sb.tile([P, T], F32)
+        nc.vector.tensor_tensor(cc[:], c0[:], f2[:], ALU.subtract)
+        v = sb.tile([P, I], F32)
+        nc.vector.tensor_tensor(v[:], aa_picked[:], bb_picked[:], ALU.max)
+        for h in range(2):
+            cols = slice(h * half, (h + 1) * half)
+            picked = gather(f"cc_picked{h}", cc, idx6, h * half, half)
+            y = sb.tile([P, half], F32, name=f"y{h}")
+            nc.vector.tensor_tensor(y[:], v[:, cols], picked[:], ALU.subtract)
+            nc.sync.dma_start(out[:, cols], y[:])

@@ -1,6 +1,7 @@
 from contextlib import ExitStack
 
 import concourse.mybir as mybir
+from concourse.masks import make_identity
 
 D, K, T, I, Q = 512, 512, 1024, 512, 128
 FLOPS = 2 * Q * (D * K + 3 * 512 * T)
@@ -52,7 +53,8 @@ def tile_attend_rotation_madethree_kernel(
         wq_plane = sb.tile([P, K], U8, align_bytes=64)
         keys_plane = sb.tile([P, T], U8, align_bytes=64)
         notes_plane = sb.tile([P, T], U8, align_bytes=64)
-        nc.vector.memset(wq_plane[:].bitcast(U32), 0)
+        identity = sb.tile([P, P], F32)
+        make_identity(nc, identity[:])
         f3 = sb.tile([P, T], F32)
         f1 = sb.tile([P, T], F32)
         f2 = sb.tile([P, T], F32)
@@ -61,10 +63,10 @@ def tile_attend_rotation_madethree_kernel(
 
         states_raw = sb.tile([P, PACK, Q], F32)
         nc.sync.dma_start(states_raw[:], states.rearrange("(p j) q -> p j q", j=PACK))
-        load_plane(nc.scalar, users_plane, users_scales)
-        users_codes = load_words(users_words, T, "users_codes")
+        load_plane(nc.scalar, wq_plane, wq_scales)
         wq_codes = load_words(wq_words, K, "wq_codes")
-        load_plane(nc.sync, wq_plane, wq_scales)
+        users_codes = load_words(users_words, T, "users_codes")
+        load_plane(nc.sync, users_plane, users_scales)
         idx3 = load_list(offs3, "idx3")
         idx = load_list(offs, "idx")
         keys_codes = load_words(keys_words, T, "keys_codes")
@@ -87,7 +89,10 @@ def tile_attend_rotation_madethree_kernel(
             in_=states_bf[:].rearrange("p q j -> p (q j)"),
         )
 
-        def score(name, lhs_codes, lhs_plane, rhs_of_bank, rhs_plane):
+        def scalar_copy(dst, src):
+            nc.scalar.activation(dst, src, COPY)
+
+        def score(name, lhs_codes, lhs_plane, rhs_of_bank, rhs_plane, copies):
             scores = sb.tile([P, T], F32, name=name)
             banks = []
             for h in range(T // BANK):
@@ -97,12 +102,12 @@ def tile_attend_rotation_madethree_kernel(
                     out=bank[:], lhsT=lhs_codes[:].bitcast(FP8X4), lhsT_scale=lhs_plane[:],
                     rhs=rhs_of_bank(cols), rhs_scale=rhs_plane[:, cols], start=True, stop=True,
                 )
-                nc.scalar.activation(scores[:, cols], bank[:], COPY)
+                copies[h](scores[:, cols], bank[:])
                 banks.append(bank)
             return scores, banks
 
-        def gather(name, window, lst, first, count):
-            picked = sb.tile([P, count], F32, name=name)
+        def gather(name, window, lst, first, count, tag=None):
+            picked = sb.tile([P, count], F32, name=name, tag=tag or name)
             nc.scalar.activation(picked[:], window[:].indirect(slots(lst, first, count)), COPY)
             return picked
 
@@ -110,60 +115,54 @@ def tile_attend_rotation_madethree_kernel(
             nc.vector.tensor_copy(window[:].indirect(slots(lst, first, values.shape[1])), values)
 
         half = I // 2
-        quarter = I // 4
 
-        c0, c0_banks = score("c0", states_codes, states_plane, lambda cols: users_codes[:, cols].bitcast(FP8X4), users_plane)
-
-        wq_dealt = sb.tile([P, PACK, P], U32, align_bytes=64)
-        nc.vector.tensor_copy(wq_dealt[:].rearrange("p j m -> p m j"), wq_codes[:].rearrange("p (m j) -> p m j", j=PACK))
-        wq_plane_dealt = sb.tile([P, PACK, P], U8, align_bytes=64)
-        nc.vector.tensor_copy(wq_plane_dealt[:].rearrange("p j m -> p m j"), wq_plane[:].rearrange("p (m j) -> p m j", j=PACK))
-        qv_bank = ps.tile([P, PACK, Q], F32)
-        for j in range(PACK):
-            nc.tensor.matmul_mx(
-                out=qv_bank[:, j, :], lhsT=wq_dealt[:, j, :].bitcast(FP8X4), lhsT_scale=wq_plane_dealt[:, j, :],
-                rhs=states_codes[:].bitcast(FP8X4), rhs_scale=states_plane[:], start=True, stop=True,
-            )
-
-        c0_first = gather("c0_first", c0, idx3, 0, half)
-        qv_bf = sb.tile([P, Q, PACK], BF16, align_bytes=64)
-        nc.scalar.copy(qv_bf[:], qv_bank[:].rearrange("p j q -> p q j"))
-        scatter(f3, idx, 0, c0_first[:, :quarter])
+        qv_bank = ps.tile([P, K], F32)
+        nc.tensor.matmul_mx(
+            out=qv_bank[:], lhsT=states_codes[:].bitcast(FP8X4), lhsT_scale=states_plane[:],
+            rhs=wq_codes[:].bitcast(FP8X4), rhs_scale=wq_plane[:], start=True, stop=True,
+        )
+        qv_rows = sb.tile([P, 2, P, 2], BF16)
+        nc.vector.tensor_copy(qv_rows[:], qv_bank[:].rearrange("q (p u e) -> q u p e", u=2, e=2))
+        qv_pairs = qv_rows[:].rearrange("q u p e -> q (u p e)").bitcast(F32)
+        turned = ps.tile([P, 2, Q], F32)
+        for u in range(2):
+            nc.tensor.transpose(turned[:, u, :], qv_pairs[:, u * P : (u + 1) * P], identity[:])
+        qv_bf = sb.tile([P, Q * PACK], BF16, align_bytes=64)
+        nc.vector.tensor_copy(qv_bf[:].bitcast(F32).rearrange("p (q u) -> p q u", u=2), turned[:].rearrange("p u q -> p q u"))
         qv_codes = sb.tile([P, Q], U32, align_bytes=64)
         qv_plane = sb.tile([P, Q], U8, align_bytes=64)
-        nc.vector.quantize_mx(
-            out=qv_codes[:].bitcast(FP8X4),
-            scales=qv_plane[:],
-            in_=qv_bf[:].rearrange("p q j -> p (q j)"),
-        )
-        scatter(f3, idx, quarter, c0_first[:, quarter:])
-        c0_second = gather("c0_second", c0, idx3, half, half)
-        scatter(f3, idx, half, c0_second[:])
+        nc.vector.quantize_mx(out=qv_codes[:].bitcast(FP8X4), scales=qv_plane[:], in_=qv_bf[:])
 
-        a, a_banks = score("a", qv_codes, qv_plane, lambda cols: keys_codes[:, cols].bitcast(FP8X4), keys_plane)
+        c0, c0_banks = score("c0", states_codes, states_plane, lambda cols: users_codes[:, cols].bitcast(FP8X4), users_plane, (scalar_copy, scalar_copy))
+        for h in range(2):
+            picked = gather(f"c0_picked{h}", c0, idx3, h * half, half)
+            scatter(f3, idx, h * half, picked[:])
+
+        a, a_banks = score("a", qv_codes, qv_plane, lambda cols: keys_codes[:, cols].bitcast(FP8X4), keys_plane, (scalar_copy, scalar_copy))
         for h in range(2):
             picked = gather(f"a_picked{h}", a, idx, h * half, half)
             scatter(f1, idx2, h * half, picked[:])
         aa = sb.tile([P, T], F32)
         nc.gpsimd.tensor_tensor(aa[:], a[:], f3[:], ALU.add)
 
-        b, b_banks = score("b", qv_codes, qv_plane, lambda cols: notes_codes[:, 2 * cols.start : 2 * cols.stop].bitcast(FP4X4), notes_plane)
+        b, b_banks = score("b", qv_codes, qv_plane, lambda cols: notes_codes[:, 2 * cols.start : 2 * cols.stop].bitcast(FP4X4), notes_plane, (scalar_copy, scalar_copy))
         for h in range(2):
             picked = gather(f"b_picked{h}", b, idx2, h * half, half)
             scatter(f2, idx3, h * half, picked[:])
-        bb = sb.tile([P, T], F32)
+        bb = sb.tile([P, T], F32, tag="bb")
         nc.gpsimd.tensor_tensor(bb[:], b[:], f1[:], ALU.add)
 
-        aa_picked = gather("aa_picked", aa, idx4, 0, I)
+        aa_picked = gather("aa_picked", aa, idx4, 0, I, tag="b_picked0")
         bb_picked = gather("bb_picked", bb, idx5, 0, I)
 
         cc = sb.tile([P, T], F32)
         nc.vector.tensor_tensor(cc[:], c0[:], f2[:], ALU.subtract)
         v = sb.tile([P, I], F32)
         nc.vector.tensor_tensor(v[:], aa_picked[:], bb_picked[:], ALU.max)
+        cc_picked = sb.tile([P, I], F32, tag="bb")
         for h in range(2):
             cols = slice(h * half, (h + 1) * half)
-            picked = gather(f"cc_picked{h}", cc, idx6, h * half, half)
+            scalar_copy(cc_picked[:, cols], cc[:].indirect(slots(idx6, h * half, half)))
             y = sb.tile([P, half], F32, name=f"y{h}")
-            nc.vector.tensor_tensor(y[:], v[:, cols], picked[:], ALU.subtract)
+            nc.vector.tensor_tensor(y[:], v[:, cols], cc_picked[:, cols], ALU.subtract)
             nc.sync.dma_start(out[:, cols], y[:])

@@ -21,6 +21,7 @@ P = 128
 PACK = 4
 BANK = 512
 PER_COLUMN = 16
+SPLIT = 768
 
 
 def tile_attend_rotation_madethree_kernel(
@@ -114,6 +115,11 @@ def tile_attend_rotation_madethree_kernel(
         def scatter(window, lst, first, values):
             nc.vector.tensor_copy(window[:].indirect(slots(lst, first, values.shape[1])), values)
 
+        def combine(dst, banks, scores, window, op):
+            nc.vector.tensor_tensor(dst[:, :BANK], banks[0][:], window[:, :BANK], op)
+            nc.vector.tensor_tensor(dst[:, BANK:SPLIT], banks[1][:, : SPLIT - BANK], window[:, BANK:SPLIT], op)
+            nc.gpsimd.tensor_tensor(dst[:, SPLIT:], scores[:, SPLIT:], window[:, SPLIT:], op)
+
         half = I // 2
 
         qv_bank = ps.tile([P, K], F32)
@@ -134,29 +140,28 @@ def tile_attend_rotation_madethree_kernel(
         nc.vector.quantize_mx(out=qv_codes[:].bitcast(FP8X4), scales=qv_plane[:], in_=qv_bf[:])
 
         c0, c0_banks = score("c0", states_codes, states_plane, lambda cols: users_codes[:, cols].bitcast(FP8X4), users_plane, (scalar_copy, scalar_copy))
-        for h in range(2):
-            picked = gather(f"c0_picked{h}", c0, idx3, h * half, half)
-            scatter(f3, idx, h * half, picked[:])
+        c0_picked = sb.tile([P, I], F32)
+        scalar_copy(c0_picked[:, :half], c0[:].indirect(slots(idx3, 0, half)))
+        nc.vector.tensor_copy(c0_picked[:, half:], c0[:].indirect(slots(idx3, half, half)))
+        scatter(f3, idx, 0, c0_picked[:])
 
         a, a_banks = score("a", qv_codes, qv_plane, lambda cols: keys_codes[:, cols].bitcast(FP8X4), keys_plane, (scalar_copy, scalar_copy))
-        for h in range(2):
-            picked = gather(f"a_picked{h}", a, idx, h * half, half)
-            scatter(f1, idx2, h * half, picked[:])
+        a_picked = gather("a_picked", a, idx, 0, I)
+        scatter(f1, idx2, 0, a_picked[:])
         aa = sb.tile([P, T], F32)
-        nc.gpsimd.tensor_tensor(aa[:], a[:], f3[:], ALU.add)
+        combine(aa, a_banks, a, f3, ALU.add)
 
         b, b_banks = score("b", qv_codes, qv_plane, lambda cols: notes_codes[:, 2 * cols.start : 2 * cols.stop].bitcast(FP4X4), notes_plane, (scalar_copy, scalar_copy))
-        for h in range(2):
-            picked = gather(f"b_picked{h}", b, idx2, h * half, half)
-            scatter(f2, idx3, h * half, picked[:])
+        b_picked = gather("b_picked", b, idx2, 0, I)
+        scatter(f2, idx3, 0, b_picked[:])
         bb = sb.tile([P, T], F32, tag="bb")
-        nc.gpsimd.tensor_tensor(bb[:], b[:], f1[:], ALU.add)
+        combine(bb, b_banks, b, f1, ALU.add)
 
-        aa_picked = gather("aa_picked", aa, idx4, 0, I, tag="b_picked0")
+        aa_picked = gather("aa_picked", aa, idx4, 0, I)
         bb_picked = gather("bb_picked", bb, idx5, 0, I)
 
         cc = sb.tile([P, T], F32)
-        nc.vector.tensor_tensor(cc[:], c0[:], f2[:], ALU.subtract)
+        combine(cc, c0_banks, c0, f2, ALU.subtract)
         v = sb.tile([P, I], F32)
         nc.vector.tensor_tensor(v[:], aa_picked[:], bb_picked[:], ALU.max)
         cc_picked = sb.tile([P, I], F32, tag="bb")

@@ -38,13 +38,13 @@ def tile_attend_rotation_madethree_kernel(
             nc.sync.dma_start(tile[:], src)
             return tile
 
-        def load_plane(queue, plane, src):
-            for r in range(4):
-                queue.dma_start(plane[r:P:32, :].bitcast(I32), src[0, r:16:4, :].bitcast(I32))
+        def load_plane(queues, plane, src, rows=range(4)):
+            for r in rows:
+                queues[r % len(queues)].dma_start(plane[r:P:32, :].bitcast(I32), src[0, r:16:4, :].bitcast(I32))
 
-        def load_words(src, columns, name):
+        def load_words(src, columns, name, queue=nc.sync):
             tile = sb.tile([P, columns], U32, name=name, align_bytes=64)
-            nc.sync.dma_start(tile[:].bitcast(I32), src[0].rearrange("p n t -> p (n t)").bitcast(I32))
+            queue.dma_start(tile[:].bitcast(I32), src[0].rearrange("p n t -> p (n t)").bitcast(I32))
             return tile
 
         def slots(lst, first, count):
@@ -63,19 +63,20 @@ def tile_attend_rotation_madethree_kernel(
             nc.vector.memset(window[:], 0.0)
 
         states_raw = sb.tile([P, PACK, Q], F32)
+        load_plane((nc.sync, nc.scalar), wq_plane, wq_scales)
         nc.sync.dma_start(states_raw[:], states.rearrange("(p j) q -> p j q", j=PACK))
-        load_plane(nc.scalar, wq_plane, wq_scales)
-        wq_codes = load_words(wq_words, K, "wq_codes")
+        wq_codes = load_words(wq_words, K, "wq_codes", nc.scalar)
         users_codes = load_words(users_words, T, "users_codes")
-        load_plane(nc.sync, users_plane, users_scales)
+        load_plane((nc.scalar,), users_plane, users_scales, range(1))
+        load_plane((nc.sync,), users_plane, users_scales, range(1, 4))
         idx3 = load_list(offs3, "idx3")
         idx = load_list(offs, "idx")
         keys_codes = load_words(keys_words, T, "keys_codes")
-        load_plane(nc.sync, keys_plane, keys_scales)
+        load_plane((nc.sync,), keys_plane, keys_scales)
         idx2 = load_list(offs2, "idx2")
         notes_codes = sb.tile([P, 2 * T], U8, align_bytes=64)
         nc.sync.dma_start(notes_codes[:].bitcast(I32), notes_words[0].bitcast(I32))
-        load_plane(nc.sync, notes_plane, notes_scales)
+        load_plane((nc.sync,), notes_plane, notes_scales)
         idx4 = load_list(offs4, "idx4")
         idx5 = load_list(offs5, "idx5")
         idx6 = load_list(offs6, "idx6")
@@ -93,17 +94,16 @@ def tile_attend_rotation_madethree_kernel(
         def scalar_copy(dst, src):
             nc.scalar.activation(dst, src, COPY)
 
-        def score(name, lhs_codes, lhs_plane, rhs_of_bank, rhs_plane, copies):
+        def score(name, lhs_codes, lhs_plane, rhs_of_bank, rhs_plane, pieces):
             scores = sb.tile([P, T], F32, name=name)
             banks = []
-            for h in range(T // BANK):
-                cols = slice(h * BANK, (h + 1) * BANK)
-                bank = ps.tile([P, BANK], F32, name=f"{name}_bank{h}")
+            for cols, tag, copy_out in pieces:
+                bank = ps.tile([P, cols.stop - cols.start], F32, name=f"{name}_{cols.start}", tag=tag)
                 nc.tensor.matmul_mx(
                     out=bank[:], lhsT=lhs_codes[:].bitcast(FP8X4), lhsT_scale=lhs_plane[:],
                     rhs=rhs_of_bank(cols), rhs_scale=rhs_plane[:, cols], start=True, stop=True,
                 )
-                copies[h](scores[:, cols], bank[:])
+                copy_out(scores[:, cols], bank[:])
                 banks.append(bank)
             return scores, banks
 
@@ -117,7 +117,7 @@ def tile_attend_rotation_madethree_kernel(
 
         def combine(dst, banks, scores, window, op):
             nc.vector.tensor_tensor(dst[:, :BANK], banks[0][:], window[:, :BANK], op)
-            nc.vector.tensor_tensor(dst[:, BANK:SPLIT], banks[1][:, : SPLIT - BANK], window[:, BANK:SPLIT], op)
+            nc.vector.tensor_tensor(dst[:, BANK:SPLIT], banks[1][:], window[:, BANK:SPLIT], op)
             nc.gpsimd.tensor_tensor(dst[:, SPLIT:], scores[:, SPLIT:], window[:, SPLIT:], op)
 
         half = I // 2
@@ -139,23 +139,33 @@ def tile_attend_rotation_madethree_kernel(
         qv_plane = sb.tile([P, Q], U8, align_bytes=64)
         nc.vector.quantize_mx(out=qv_codes[:].bitcast(FP8X4), scales=qv_plane[:], in_=qv_bf[:])
 
-        c0, c0_banks = score("c0", states_codes, states_plane, lambda cols: users_codes[:, cols].bitcast(FP8X4), users_plane, (scalar_copy, scalar_copy))
+        c0, c0_banks = score("c0", states_codes, states_plane, lambda cols: users_codes[:, cols].bitcast(FP8X4), users_plane, (
+            (slice(0, BANK), "c0_0", scalar_copy),
+            (slice(BANK, SPLIT), "c0_1", scalar_copy),
+            (slice(SPLIT, T), "c0_2", nc.vector.tensor_copy),
+        ))
         c0_picked = sb.tile([P, I], F32)
         scalar_copy(c0_picked[:, :half], c0[:].indirect(slots(idx3, 0, half)))
         nc.vector.tensor_copy(c0_picked[:, half:], c0[:].indirect(slots(idx3, half, half)))
         scatter(f3, idx, 0, c0_picked[:])
 
-        a, a_banks = score("a", qv_codes, qv_plane, lambda cols: keys_codes[:, cols].bitcast(FP8X4), keys_plane, (scalar_copy, scalar_copy))
+        a, a_banks = score("a", qv_codes, qv_plane, lambda cols: keys_codes[:, cols].bitcast(FP8X4), keys_plane, (
+            (slice(0, BANK), "a_0", scalar_copy),
+            (slice(BANK, T), "a_1", scalar_copy),
+        ))
         a_picked = gather("a_picked", a, idx, 0, I)
         scatter(f1, idx2, 0, a_picked[:])
-        aa = sb.tile([P, T], F32)
-        combine(aa, a_banks, a, f3, ALU.add)
 
-        b, b_banks = score("b", qv_codes, qv_plane, lambda cols: notes_codes[:, 2 * cols.start : 2 * cols.stop].bitcast(FP4X4), notes_plane, (scalar_copy, scalar_copy))
+        b, b_banks = score("b", qv_codes, qv_plane, lambda cols: notes_codes[:, 2 * cols.start : 2 * cols.stop].bitcast(FP4X4), notes_plane, (
+            (slice(0, BANK), "b_0", scalar_copy),
+            (slice(BANK, T), "qv_bank", scalar_copy),
+        ))
         b_picked = gather("b_picked", b, idx2, 0, I)
         scatter(f2, idx3, 0, b_picked[:])
+        aa = sb.tile([P, T], F32, align_bytes=64, tag="notes_codes")
+        nc.gpsimd.tensor_tensor(aa[:], a[:], f3[:], ALU.add)
         bb = sb.tile([P, T], F32, tag="bb")
-        combine(bb, b_banks, b, f1, ALU.add)
+        nc.gpsimd.tensor_tensor(bb[:], b[:], f1[:], ALU.add)
 
         aa_picked = gather("aa_picked", aa, idx4, 0, I)
         bb_picked = gather("bb_picked", bb, idx5, 0, I)
@@ -165,9 +175,10 @@ def tile_attend_rotation_madethree_kernel(
         v = sb.tile([P, I], F32)
         nc.vector.tensor_tensor(v[:], aa_picked[:], bb_picked[:], ALU.max)
         cc_picked = sb.tile([P, I], F32, tag="bb")
+        scalar_copy(cc_picked[:, :half], cc[:].indirect(slots(idx6, 0, half)))
+        nc.vector.tensor_copy(cc_picked[:, half:], cc[:].indirect(slots(idx6, half, half)))
         for h in range(2):
             cols = slice(h * half, (h + 1) * half)
-            scalar_copy(cc_picked[:, cols], cc[:].indirect(slots(idx6, h * half, half)))
             y = sb.tile([P, half], F32, name=f"y{h}")
             nc.vector.tensor_tensor(y[:], v[:, cols], cc_picked[:, cols], ALU.subtract)
             nc.sync.dma_start(out[:, cols], y[:])

@@ -1,7 +1,6 @@
 from contextlib import ExitStack
 
 import concourse.mybir as mybir
-from concourse.masks import make_identity
 
 D, K, T, I, Q = 512, 512, 1024, 512, 128
 FLOPS = 2 * Q * (D * K + 3 * 512 * T)
@@ -47,6 +46,9 @@ def tile_attend_rotation_madethree_kernel(
             queue.dma_start(tile[:].bitcast(I32), src[0].rearrange("p n t -> p (n t)").bitcast(I32))
             return tile
 
+        def scalar_copy(dst, src):
+            nc.scalar.activation(dst, src, COPY)
+
         def slots(lst, first, count):
             return lst[:, first // PER_COLUMN : (first + count) // PER_COLUMN]
 
@@ -54,8 +56,7 @@ def tile_attend_rotation_madethree_kernel(
         wq_plane = sb.tile([P, K], U8, align_bytes=64)
         keys_plane = sb.tile([P, T], U8, align_bytes=64)
         notes_plane = sb.tile([P, T], U8, align_bytes=64)
-        identity = sb.tile([P, P], F32)
-        make_identity(nc, identity[:])
+        nc.vector.memset(wq_plane[:].bitcast(U32), 0)
         f3 = sb.tile([P, T], F32)
         f1 = sb.tile([P, T], F32)
         f2 = sb.tile([P, T], F32)
@@ -65,11 +66,11 @@ def tile_attend_rotation_madethree_kernel(
         states_raw = sb.tile([P, PACK, Q], F32)
         load_plane((nc.sync, nc.scalar), wq_plane, wq_scales)
         nc.sync.dma_start(states_raw[:], states.rearrange("(p j) q -> p j q", j=PACK))
-        wq_codes = load_words(wq_words, K, "wq_codes", nc.scalar)
+        wq_codes = load_words(wq_words, K, "wq_codes")
         users_codes = load_words(users_words, T, "users_codes")
-        load_plane((nc.scalar,), users_plane, users_scales, range(1))
-        load_plane((nc.sync,), users_plane, users_scales, range(1, 4))
+        load_plane((nc.sync,), users_plane, users_scales, range(1))
         idx3 = load_list(offs3, "idx3")
+        load_plane((nc.sync,), users_plane, users_scales, range(1, 4))
         idx = load_list(offs, "idx")
         keys_codes = load_words(keys_words, T, "keys_codes")
         load_plane((nc.sync,), keys_plane, keys_scales)
@@ -82,7 +83,11 @@ def tile_attend_rotation_madethree_kernel(
         idx6 = load_list(offs6, "idx6")
 
         states_bf = sb.tile([P, Q, PACK], BF16, align_bytes=64)
-        nc.vector.tensor_copy(states_bf[:], states_raw[:].rearrange("p j q -> p q j"))
+        wq_plane_dealt = sb.tile([P, PACK, P], U8, align_bytes=64)
+        nc.vector.tensor_copy(wq_plane_dealt[:].rearrange("p j m -> p m j"), wq_plane[:].rearrange("p (m j) -> p m j", j=PACK))
+        states_turned = states_raw[:].rearrange("p j q -> p q j")
+        nc.vector.tensor_copy(states_bf[:, : Q // 2, :], states_turned[:, : Q // 2, :])
+        scalar_copy(states_bf[:, Q // 2 :, :], states_turned[:, Q // 2 :, :])
         states_codes = sb.tile([P, Q], U32, align_bytes=64)
         states_plane = sb.tile([P, Q], U8, align_bytes=64)
         nc.vector.quantize_mx(
@@ -90,9 +95,6 @@ def tile_attend_rotation_madethree_kernel(
             scales=states_plane[:],
             in_=states_bf[:].rearrange("p q j -> p (q j)"),
         )
-
-        def scalar_copy(dst, src):
-            nc.scalar.activation(dst, src, COPY)
 
         def score(name, lhs_codes, lhs_plane, rhs_of_bank, rhs_plane, pieces):
             scores = sb.tile([P, T], F32, name=name)
@@ -122,19 +124,16 @@ def tile_attend_rotation_madethree_kernel(
 
         half = I // 2
 
-        qv_bank = ps.tile([P, K], F32)
-        nc.tensor.matmul_mx(
-            out=qv_bank[:], lhsT=states_codes[:].bitcast(FP8X4), lhsT_scale=states_plane[:],
-            rhs=wq_codes[:].bitcast(FP8X4), rhs_scale=wq_plane[:], start=True, stop=True,
-        )
-        qv_rows = sb.tile([P, 2, P, 2], BF16)
-        nc.vector.tensor_copy(qv_rows[:], qv_bank[:].rearrange("q (p u e) -> q u p e", u=2, e=2))
-        qv_pairs = qv_rows[:].rearrange("q u p e -> q (u p e)").bitcast(F32)
-        turned = ps.tile([P, 2, Q], F32)
-        for u in range(2):
-            nc.tensor.transpose(turned[:, u, :], qv_pairs[:, u * P : (u + 1) * P], identity[:])
+        wq_dealt = sb.tile([P, PACK, P], U32, align_bytes=64)
+        nc.scalar.copy(wq_dealt[:].rearrange("p j m -> p m j"), wq_codes[:].rearrange("p (m j) -> p m j", j=PACK))
+        qv_bank = ps.tile([P, PACK, Q], F32)
+        for j in range(PACK):
+            nc.tensor.matmul_mx(
+                out=qv_bank[:, j, :], lhsT=wq_dealt[:, j, :].bitcast(FP8X4), lhsT_scale=wq_plane_dealt[:, j, :],
+                rhs=states_codes[:].bitcast(FP8X4), rhs_scale=states_plane[:], start=True, stop=True,
+            )
         qv_bf = sb.tile([P, Q * PACK], BF16, align_bytes=64)
-        nc.vector.tensor_copy(qv_bf[:].bitcast(F32).rearrange("p (q u) -> p q u", u=2), turned[:].rearrange("p u q -> p q u"))
+        nc.vector.tensor_copy(qv_bf[:].rearrange("p (q j) -> p q j", j=PACK), qv_bank[:].rearrange("p j q -> p q j"))
         qv_codes = sb.tile([P, Q], U32, align_bytes=64)
         qv_plane = sb.tile([P, Q], U8, align_bytes=64)
         nc.vector.quantize_mx(out=qv_codes[:].bitcast(FP8X4), scales=qv_plane[:], in_=qv_bf[:])

from contextlib import ExitStack

import concourse.mybir as mybir

D, K, T, I, Q = 512, 512, 1024, 512, 128
FLOPS = 2 * Q * (D * K + 3 * 512 * T)

F32 = mybir.dt.float32
BF16 = mybir.dt.bfloat16
I32 = mybir.dt.int32
U32 = mybir.dt.uint32
U16 = mybir.dt.uint16
U8 = mybir.dt.uint8
FP8X4 = mybir.dt.float8_e4m3fn_x4
FP4X4 = mybir.dt.float4_e2m1fn_x4
COPY = mybir.ActivationFunctionType.Copy
ALU = mybir.AluOpType

P = 128
PACK = 4
BANK = 512
PER_COLUMN = 16
SPLIT = 768


def tile_attend_rotation_madethree_kernel(
    tc, states, wq_words, wq_scales, keys_words, keys_scales, notes_words, notes_scales,
    users_words, users_scales, offs, offs2, offs3, offs4, offs5, offs6, out,
):
    nc = tc.nc
    with ExitStack() as ctx:
        sb = ctx.enter_context(tc.tile_pool(name="sb", bufs=1))
        ps = ctx.enter_context(tc.psum_pool(name="ps", bufs=1))

        def load_list(src, name):
            tile = sb.tile([P, I // PER_COLUMN], U16, name=name)
            nc.sync.dma_start(tile[:], src)
            return tile

        def load_plane(queues, plane, src, rows=range(4)):
            for r in rows:
                queues[r % len(queues)].dma_start(plane[r:P:32, :].bitcast(I32), src[0, r:16:4, :].bitcast(I32))

        def load_words(src, columns, name, queue=nc.sync):
            tile = sb.tile([P, columns], U32, name=name, align_bytes=64)
            queue.dma_start(tile[:].bitcast(I32), src[0].rearrange("p n t -> p (n t)").bitcast(I32))
            return tile

        def scalar_copy(dst, src):
            nc.scalar.activation(dst, src, COPY)

        def slots(lst, first, count):
            return lst[:, first // PER_COLUMN : (first + count) // PER_COLUMN]

        users_plane = sb.tile([P, T], U8, align_bytes=64)
        wq_plane = sb.tile([P, K], U8, align_bytes=64)
        keys_plane = sb.tile([P, T], U8, align_bytes=64)
        notes_plane = sb.tile([P, T], U8, align_bytes=64)
        nc.vector.memset(wq_plane[:].bitcast(U32), 0)
        f3 = sb.tile([P, T], F32)
        f1 = sb.tile([P, T], F32)
        f2 = sb.tile([P, T], F32)
        for window in (f3, f1, f2):
            nc.vector.memset(window[:], 0.0)

        states_raw = sb.tile([P, PACK, Q], F32)
        load_plane((nc.sync, nc.scalar), wq_plane, wq_scales)
        nc.sync.dma_start(states_raw[:], states.rearrange("(p j) q -> p j q", j=PACK))
        wq_codes = load_words(wq_words, K, "wq_codes")
        users_codes = load_words(users_words, T, "users_codes")
        load_plane((nc.sync,), users_plane, users_scales, range(1))
        idx3 = load_list(offs3, "idx3")
        load_plane((nc.sync,), users_plane, users_scales, range(1, 4))
        idx = load_list(offs, "idx")
        keys_codes = load_words(keys_words, T, "keys_codes")
        load_plane((nc.sync,), keys_plane, keys_scales)
        idx2 = load_list(offs2, "idx2")
        notes_codes = sb.tile([P, 2 * T], U8, align_bytes=64)
        nc.sync.dma_start(notes_codes[:].bitcast(I32), notes_words[0].bitcast(I32))
        load_plane((nc.sync,), notes_plane, notes_scales)
        idx4 = load_list(offs4, "idx4")
        idx5 = load_list(offs5, "idx5")
        idx6 = load_list(offs6, "idx6")

        states_bf = sb.tile([P, Q, PACK], BF16, align_bytes=64)
        wq_plane_dealt = sb.tile([P, PACK, P], U8, align_bytes=64)
        nc.vector.tensor_copy(wq_plane_dealt[:].rearrange("p j m -> p m j"), wq_plane[:].rearrange("p (m j) -> p m j", j=PACK))
        states_turned = states_raw[:].rearrange("p j q -> p q j")
        nc.vector.tensor_copy(states_bf[:, : Q // 2, :], states_turned[:, : Q // 2, :])
        scalar_copy(states_bf[:, Q // 2 :, :], states_turned[:, Q // 2 :, :])
        states_codes = sb.tile([P, Q], U32, align_bytes=64)
        states_plane = sb.tile([P, Q], U8, align_bytes=64)
        nc.vector.quantize_mx(
            out=states_codes[:].bitcast(FP8X4),
            scales=states_plane[:],
            in_=states_bf[:].rearrange("p q j -> p (q j)"),
        )

        def score(name, lhs_codes, lhs_plane, rhs_of_bank, rhs_plane, pieces):
            scores = sb.tile([P, T], F32, name=name)
            banks = []
            for cols, tag, copy_out in pieces:
                bank = ps.tile([P, cols.stop - cols.start], F32, name=f"{name}_{cols.start}", tag=tag)
                nc.tensor.matmul_mx(
                    out=bank[:], lhsT=lhs_codes[:].bitcast(FP8X4), lhsT_scale=lhs_plane[:],
                    rhs=rhs_of_bank(cols), rhs_scale=rhs_plane[:, cols], start=True, stop=True,
                )
                copy_out(scores[:, cols], bank[:])
                banks.append(bank)
            return scores, banks

        def gather(name, window, lst, first, count, tag=None):
            picked = sb.tile([P, count], F32, name=name, tag=tag or name)
            nc.scalar.activation(picked[:], window[:].indirect(slots(lst, first, count)), COPY)
            return picked

        def scatter(window, lst, first, values):
            nc.vector.tensor_copy(window[:].indirect(slots(lst, first, values.shape[1])), values)

        def combine(dst, banks, scores, window, op):
            nc.vector.tensor_tensor(dst[:, :BANK], banks[0][:], window[:, :BANK], op)
            nc.vector.tensor_tensor(dst[:, BANK:SPLIT], banks[1][:], window[:, BANK:SPLIT], op)
            nc.gpsimd.tensor_tensor(dst[:, SPLIT:], scores[:, SPLIT:], window[:, SPLIT:], op)

        half = I // 2

        wq_dealt = sb.tile([P, PACK, P], U32, align_bytes=64)
        nc.scalar.copy(wq_dealt[:].rearrange("p j m -> p m j"), wq_codes[:].rearrange("p (m j) -> p m j", j=PACK))
        qv_bank = ps.tile([P, PACK, Q], F32)
        for j in range(PACK):
            nc.tensor.matmul_mx(
                out=qv_bank[:, j, :], lhsT=wq_dealt[:, j, :].bitcast(FP8X4), lhsT_scale=wq_plane_dealt[:, j, :],
                rhs=states_codes[:].bitcast(FP8X4), rhs_scale=states_plane[:], start=True, stop=True,
            )
        qv_bf = sb.tile([P, Q * PACK], BF16, align_bytes=64)
        nc.vector.tensor_copy(qv_bf[:].rearrange("p (q j) -> p q j", j=PACK), qv_bank[:].rearrange("p j q -> p q j"))
        qv_codes = sb.tile([P, Q], U32, align_bytes=64)
        qv_plane = sb.tile([P, Q], U8, align_bytes=64)
        nc.vector.quantize_mx(out=qv_codes[:].bitcast(FP8X4), scales=qv_plane[:], in_=qv_bf[:])

        c0, c0_banks = score("c0", states_codes, states_plane, lambda cols: users_codes[:, cols].bitcast(FP8X4), users_plane, (
            (slice(0, BANK), "c0_0", scalar_copy),
            (slice(BANK, SPLIT), "c0_1", scalar_copy),
            (slice(SPLIT, T), "c0_2", nc.vector.tensor_copy),
        ))
        c0_picked = sb.tile([P, I], F32)
        scalar_copy(c0_picked[:, :half], c0[:].indirect(slots(idx3, 0, half)))
        nc.vector.tensor_copy(c0_picked[:, half:], c0[:].indirect(slots(idx3, half, half)))
        scatter(f3, idx, 0, c0_picked[:])

        a, a_banks = score("a", qv_codes, qv_plane, lambda cols: keys_codes[:, cols].bitcast(FP8X4), keys_plane, (
            (slice(0, BANK), "a_0", scalar_copy),
            (slice(BANK, T), "a_1", scalar_copy),
        ))
        a_picked = gather("a_picked", a, idx, 0, I)
        scatter(f1, idx2, 0, a_picked[:])

        b, b_banks = score("b", qv_codes, qv_plane, lambda cols: notes_codes[:, 2 * cols.start : 2 * cols.stop].bitcast(FP4X4), notes_plane, (
            (slice(0, BANK), "b_0", scalar_copy),
            (slice(BANK, T), "qv_bank", scalar_copy),
        ))
        b_picked = gather("b_picked", b, idx2, 0, I)
        scatter(f2, idx3, 0, b_picked[:])
        aa = sb.tile([P, T], F32, align_bytes=64, tag="notes_codes")
        nc.gpsimd.tensor_tensor(aa[:], a[:], f3[:], ALU.add)
        bb = sb.tile([P, T], F32, tag="bb")
        nc.gpsimd.tensor_tensor(bb[:], b[:], f1[:], ALU.add)

        aa_picked = gather("aa_picked", aa, idx4, 0, I)
        bb_picked = gather("bb_picked", bb, idx5, 0, I)

        cc = sb.tile([P, T], F32)
        combine(cc, c0_banks, c0, f2, ALU.subtract)
        v = sb.tile([P, I], F32)
        nc.vector.tensor_tensor(v[:], aa_picked[:], bb_picked[:], ALU.max)
        cc_picked = sb.tile([P, I], F32, tag="bb")
        scalar_copy(cc_picked[:, :half], cc[:].indirect(slots(idx6, 0, half)))
        nc.vector.tensor_copy(cc_picked[:, half:], cc[:].indirect(slots(idx6, half, half)))
        for h in range(2):
            cols = slice(h * half, (h + 1) * half)
            y = sb.tile([P, half], F32, name=f"y{h}")
            nc.vector.tensor_tensor(y[:], v[:, cols], cc_picked[:, cols], ALU.subtract)
            nc.sync.dma_start(out[:, cols], y[:])
